import numpy as np, ml_dtypes
CORES = [50,52,122,124]
N = 4
import mx_ref
NC, G = 256, 4
C = np.float32(0.023)
BF = ml_dtypes.bfloat16
def cut(t, i, w=512):
    return t[:, w * i:w * i + w]
def tile(rs):
    return np.stack(rs, axis=2).reshape(128, -1).astype(BF)
def layer(w, X):
    out = []
    for i in range(G):
        for t in range(len(X)):
            p = mx_ref.matmul(mx_ref.quantize(cut(w, len(X) * i + t)), X[t])
            z = p if t == 0 else z + p
        out.append(z)
    return out
def act(Z):
    return [np.maximum(z, 0) * C for z in Z]
def pick(b):
    s = np.zeros((128, 128, 4), np.float32)
    s[np.arange(128), np.arange(128), b] = 1.0
    return mx_ref.quantize(s.reshape(128, 512).astype(BF))
def setup_inputs(rng):
    def f(*shape):
        return mx_ref.flush((rng.standard_normal(shape, dtype=np.float32) * np.exp2(rng.integers(-2, 3, shape[:-1] + (1,)))).astype(BF))
    return {"a": f(N, 128, G * 512), "b": f(N, 128, N * 4 * NC)}
def setup_inputs_blocks(rng):
    d = setup_inputs(rng)
    for k in ("a", "b"): d[k] = mx_ref.spread(d[k], rng, 4)
    return d
def setup_inputs_wide(rng):
    d = setup_inputs(rng)
    for k in ("a", "b"): d[k] = mx_ref.flush((d[k].astype(np.float32) * np.exp2(rng.integers(-8, 9, (N, 1, 1))).astype(np.float32)).astype(BF))
    return d
def reference(a, b):
    S = [pick(t) for t in range(4)]
    y = np.zeros((N, 128, NC, 4), np.float32)
    for c in range(N):
        for k in range(1, N + 1):
            r = (c + k) % N
            R = act(layer(a[r], [mx_ref.quantize(cut(b[r], c, 4 * NC))]))
            if k > 1: R = [R[t] + mx_ref.matmul(S[t], q) for t in range(4)]
            if k < N: q = mx_ref.quantize(tile(R))
        y[c] = np.stack(R, axis=2)
    return {"y": y.reshape(N, 128, 4 * NC)}

@@ -1,0 +1,222 @@
+from concourse.mybir import dt, AluOpType, ActivationFunctionType
+
+N = 4
+NC = 256
+HW = 128
+CSC = 0.023
+
+SCRATCH = {
+    "a_sb": ("sbuf", [128, 2048], "bfloat16"),
+    "b_sb": ("sbuf", [128, 4096], "bfloat16"),
+    "qa": ("sbuf", [128, 512], "float8_e4m3fn_x4"),
+    "pa": ("sbuf", [128, 512], "uint8"),
+    "qb": ("sbuf", [128, 1024], "float8_e4m3fn_x4"),
+    "pb": ("sbuf", [128, 1024], "uint8"),
+    "e_sb": ("sbuf", [128, 516], "bfloat16"),
+    "qs": ("sbuf", [128, 512], "float8_e4m3fn_x4"),
+    "pS": ("sbuf", [128, 512], "uint8"),
+    "y_sb": ("sbuf", [128, 1024], "float32"),
+    "ps": ("psum", [128, 4096], "float32"),
+}
+for _k in (1, 2, 3):
+    SCRATCH["t%d" % _k] = ("sbuf", [128, 1024], "bfloat16")
+    SCRATCH["qt%d" % _k] = ("sbuf", [128, NC], "float8_e4m3fn_x4")
+    SCRATCH["pt%d" % _k] = ("sbuf", [128, NC], "uint8")
+    SCRATCH["r%d" % (_k + 1)] = ("sbuf", [128, 1024], "float32")
+    SCRATCH["qi%d" % (_k + 1)] = ("sbuf", [128, NC], "float8_e4m3fn_x4")
+    SCRATCH["pi%d" % (_k + 1)] = ("sbuf", [128, NC], "uint8")
+
+SEMAPHORES = (["la0", "la1", "lb10", "lb11", "lb2", "lb3", "lb4", "e1", "e2", "qa0", "qa1", "qb10", "qb11",
+               "qb2", "qb3", "qb4", "qS", "st0", "st1", "sent1", "sent2", "sent3", "fwd"]
+              + ["mb%d" % i for i in range(8)] + ["rg%d" % i for i in range(11)]
+              + ["qt%d%d" % (k, h) for k in (1, 2, 3) for h in (0, 1)]
+              + ["in%d%d" % (k, h) for k in (2, 3, 4) for h in (0, 1)]
+              + ["rl%d%d" % (k, h) for k in (1, 2, 3) for h in (0, 1)])
+
+
+def _engines(mask):
+    return bin(mask).count("1")
+
+
+def _relays(topo, cores, s, d):
+    if topo.may_write(s, d):
+        return None
+    cand = [c for c in range(topo.CORES_PER_CHIP * topo.CHIPS)
+            if topo.chip(c) == topo.chip(s) and c not in cores and topo.may_write(c, d)]
+    cand.sort(key=lambda c: (topo.die(c) != topo.die(s), c))
+    return cand[0], cand[1]
+
+
+def rank_program(g, core, T, topo):
+    cores = list(T.cores)
+    sem = T.sem
+
+    def put(dst, out_ap, in_ap, rsem, lsem):
+        rid, pid, _se = topo.addr(dst)
+        m = topo.mask(core, dst)
+        g.remote_dma(out_ap=out_ap, in_ap=in_ap, remote_sem=rsem, local_sem=lsem, pid=pid, routing_id=rid,
+                     dma_engine_mask=m)
+        return _engines(m)
+
+    def codes(buf, h):
+        return buf[:, HW * h:HW * h + HW].bitcast(dt.uint8)
+
+    def plane(buf, h):
+        return buf[:, HW * h:HW * h + HW]
+
+    rank = T.rank_of(core)
+    if rank is None:
+        for i in range(N):
+            s, d = cores[i], cores[(i + 1) % N]
+            rl = _relays(topo, cores, s, d)
+            if rl is None or core not in rl:
+                continue
+            got = _engines(topo.mask(s, core))
+            left = 0
+            for k in (1, 2, 3):
+                for h in (0, 1):
+                    g.wait_ge(sem["rl%d%d" % (k, h)], got)
+                    if core == rl[0]:
+                        v = codes(T["qi%d" % (k + 1)], h)
+                    else:
+                        v = plane(T["pi%d" % (k + 1)], h)
+                    left += put(d, v, v, sem["in%d%d" % (k + 1, h)], sem.fwd)
+            g.wait_ge(sem.fwd, left)
+        return
+
+    te, ve, sc, sy = g.tensor, g.vector, g.scalar, g.sync
+    nxt, prv = cores[(rank + 1) % N], cores[(rank - 1) % N]
+    out_rl = _relays(topo, cores, core, nxt)
+    in_rl = _relays(topo, cores, prv, core)
+    if in_rl is None:
+        arrive = 2 * _engines(topo.mask(prv, core))
+    else:
+        arrive = _engines(topo.mask(in_rl[0], core)) + _engines(topo.mask(in_rl[1], core))
+    if out_rl is None:
+        tgt = (nxt, nxt)
+    else:
+        tgt = out_rl
+    sent_tot = 2 * (_engines(topo.mask(core, tgt[0])) + _engines(topo.mask(core, tgt[1])))
+    chain = [None] + [(rank - k) % N for k in (1, 2, 3, 4)]
+
+    def load_b(k, lo, hi, s):
+        c0 = 1024 * chain[k]
+        sy.dma_start(T.b_sb[:, c0 + lo:c0 + hi], T.b[:, c0 + lo:c0 + hi]).then_inc(s, 16)
+
+    sy.dma_start(T.a_sb[:, 0:1024], T.a[:, 0:1024]).then_inc(sem.la0, 16)
+    sc.dma_start(T.a_sb[:, 1024:2048], T.a[:, 1024:2048]).then_inc(sem.la1, 16)
+    load_b(1, 0, 512, sem.lb10)
+    load_b(1, 512, 1024, sem.lb11)
+    load_b(2, 0, 1024, sem.lb2)
+    sy.wait_ge(sem.sent1, sent_tot)
+    load_b(3, 0, 1024, sem.lb3)
+    sy.wait_ge(sem.sent2, sent_tot)
+    load_b(4, 0, 1024, sem.lb4)
+
+    ve.memset(T.e_sb[:], 1.0).then_inc(sem.e1, 1)
+    g.wait_ge(sem.e1, 1)
+    g.affine_select(T.e_sb[:], T.e_sb[:], [[-1, 516]], AluOpType.is_equal, 0.0, 3, 4).then_inc(sem.e2, 1)
+
+    def quant_b(k, lo, hi, ls, qsem):
+        w0 = NC * chain[k]
+        ve.wait_ge(ls, 16)
+        ve.quantize_mx(T.qb[:, w0 + lo:w0 + hi], T.pb[:, w0 + lo:w0 + hi],
+                       T.b_sb[:, 4 * (w0 + lo):4 * (w0 + hi)]).then_inc(qsem, 1)
+
+    for j, (ls, qsem) in enumerate(((sem.la0, sem.qa0), (sem.la1, sem.qa1))):
+        ve.wait_ge(ls, 16)
+        ve.quantize_mx(T.qa[:, 256 * j:256 * j + 256], T.pa[:, 256 * j:256 * j + 256],
+                       T.a_sb[:, 1024 * j:1024 * j + 1024]).then_inc(qsem, 1)
+    quant_b(1, 0, HW, sem.lb10, sem.qb10)
+    quant_b(1, HW, NC, sem.lb11, sem.qb11)
+
+    st = {"gi": 0}
+    reader = [None, None]
+    mbc = [0] * 8
+
+    def group(lq, lp, rq, rp, n, pre):
+        gi = st["gi"]
+        st["gi"] += 1
+        s = gi % 2
+        if reader[s] is not None:
+            te.wait_ge(reader[s][0], reader[s][1])
+        outs = []
+        for b in range(4):
+            for w in pre.get(b, ()):
+                te.wait_ge(w[0], w[1])
+            bank = 4 * s + b
+            mbc[bank] += 1
+            o = T.ps[:, 512 * bank:512 * bank + n]
+            te.matmul_mx(o, lq[:, 128 * b:128 * b + 128], lp[:, 128 * b:128 * b + 128], rq, rp,
+                         True, True).then_inc(sem["mb%d" % bank], 1)
+            outs.append((o, sem["mb%d" % bank], mbc[bank]))
+        rg = sem["rg%d" % gi]
+        reader[s] = (rg, 4)
+        return outs, rg
+
+    def send(k, h):
+        g.wait_ge(sem["qt%d%d" % (k, h)], 1)
+        ls = sem["sent%d" % k]
+        rs = sem["in%d%d" % (k + 1, h)] if out_rl is None else sem["rl%d%d" % (k, h)]
+        put(tgt[0], codes(T["qi%d" % (k + 1)], h), codes(T["qt%d" % k], h), rs, ls)
+        put(tgt[1], plane(T["pi%d" % (k + 1)], h), plane(T["pt%d" % k], h), rs, ls)
+
+    def quant_t(k, h, rg):
+        ve.wait_ge(rg, 4)
+        ve.quantize_mx(T["qt%d" % k][:, HW * h:HW * h + HW], T["pt%d" % k][:, HW * h:HW * h + HW],
+                       T["t%d" % k][:, 512 * h:512 * h + 512]).then_inc(sem["qt%d%d" % (k, h)], 1)
+        send(k, h)
+
+    w1 = NC * chain[1]
+    rgs = []
+    for h in (0, 1):
+        pre = {0: [(sem["qb1%d" % h], 1)]}
+        if h == 0:
+            pre[0].append((sem.qa0, 1))
+            pre[2] = [(sem.qa1, 1)]
+        outs, rg = group(T.qa, T.pa, T.qb[:, w1 + HW * h:w1 + HW * h + HW], T.pb[:, w1 + HW * h:w1 + HW * h + HW],
+                         HW, pre)
+        for b, (o, ms, mc) in enumerate(outs):
+            sc.wait_ge(ms, mc)
+            sc.activation(T.t1[:, 512 * h + b:512 * h + 512:4], o, ActivationFunctionType.Relu,
+                          scale=CSC).then_inc(rg, 1)
+        rgs.append(rg)
+    for h in (0, 1):
+        quant_t(1, h, rgs[h])
+
+    ve.wait_ge(sem.e2, 1)
+    for b in range(4):
+        ve.quantize_mx(T.qs[:, 128 * b:128 * b + 128], T.pS[:, 128 * b:128 * b + 128],
+                       T.e_sb[:, 3 - b:3 - b + 512]).then_inc(sem.qS, 1)
+
+    for k in (2, 3, 4):
+        quant_b(k, 0, NC, sem["lb%d" % k], sem["qb%d" % k])
+        wk = NC * chain[k]
+        outs, rgp = group(T.qa, T.pa, T.qb[:, wk:wk + NC], T.pb[:, wk:wk + NC], NC, {0: [(sem["qb%d" % k], 1)]})
+        R = T["r%d" % k]
+        for b, (o, ms, mc) in enumerate(outs):
+            sc.wait_ge(ms, mc)
+            sc.activation(R[:, NC * b:NC * b + NC], o, ActivationFunctionType.Relu, scale=CSC).then_inc(rgp, 1)
+        dst = T.y_sb if k == 4 else T["t%d" % k]
+        for h in (0, 1):
+            pre = {0: [(sem["in%d%d" % (k, h)], arrive)]}
+            if k == 2 and h == 0:
+                pre[0].append((sem.qS, 4))
+            outs, rg = group(T.qs, T.pS, T["qi%d" % k][:, HW * h:HW * h + HW], T["pi%d" % k][:, HW * h:HW * h + HW],
+                             HW, pre)
+            if h == 0:
+                ve.wait_ge(rgp, 4)
+            for b, (o, ms, mc) in enumerate(outs):
+                ve.wait_ge(ms, mc)
+                ve.tensor_tensor(dst[:, 512 * h + b:512 * h + 512:4], R[:, NC * b + HW * h:NC * b + HW * h + HW], o,
+                                 AluOpType.add).then_inc(rg, 1)
+            if k < 4:
+                quant_t(k, h, rg)
+            else:
+                sy.wait_ge(rg, 4)
+                sy.dma_start(T.y[:, 512 * h:512 * h + 512], T.y_sb[:, 512 * h:512 * h + 512]).then_inc(
+                    sem["st%d" % h], 16)
+
+    g.wait_ge(sem.sent3, sent_tot)
+    sy.wait_ge(sem.st0, 16)
+    sy.wait_ge(sem.st1, 16)

@@ -12,9 +12,12 @@ SCRATCH = {
     "pa": ("sbuf", [128, 512], "uint8"),
     "qb": ("sbuf", [128, 1024], "float8_e4m3fn_x4"),
     "pb": ("sbuf", [128, 1024], "uint8"),
+    "o_sb": ("sbuf", [128, 128], "bfloat16"),
     "e_sb": ("sbuf", [128, 516], "bfloat16"),
     "qs": ("sbuf", [128, 512], "float8_e4m3fn_x4"),
     "pS": ("sbuf", [128, 512], "uint8"),
+    "qsi": ("sbuf", [128, 128], "float8_e4m3fn_x4"),
+    "psi": ("sbuf", [128, 128], "uint8"),
     "y_sb": ("sbuf", [128, 1024], "float32"),
     "ps": ("psum", [128, 4096], "float32"),
 }
@@ -26,8 +29,8 @@ for _k in (1, 2, 3):
     SCRATCH["qi%d" % (_k + 1)] = ("sbuf", [128, NC], "float8_e4m3fn_x4")
     SCRATCH["pi%d" % (_k + 1)] = ("sbuf", [128, NC], "uint8")
 
-SEMAPHORES = (["la0", "la1", "lb10", "lb11", "lb2", "lb3", "lb4", "e1", "e2", "qa0", "qa1", "qb10", "qb11",
-               "qb2", "qb3", "qb4", "qS", "st0", "st1", "sent1", "sent2", "sent3", "fwd"]
+SEMAPHORES = (["la0", "la1", "lb10", "lb11", "lb2", "lb3", "lb4", "e1", "e2", "e3", "qa0", "qa2", "qa3", "qb10", "qb11",
+               "qb2", "qb3", "qb4", "qS", "qS3", "sS", "sSl", "st0", "st1", "sent1", "sent2", "sent3", "fwd"]
               + ["mb%d" % i for i in range(8)] + ["rg%d" % i for i in range(11)]
               + ["qt%d%d" % (k, h) for k in (1, 2, 3) for h in (0, 1)]
               + ["in%d%d" % (k, h) for k in (2, 3, 4) for h in (0, 1)]
@@ -47,9 +50,20 @@ def _relays(topo, cores, s, d):
     return cand[0], cand[1]
 
 
+def _feeders(topo, cores, j):
+    d, prv, nxt = cores[j], cores[(j - 1) % N], cores[(j + 1) % N]
+    rl = _relays(topo, cores, prv, d)
+    fs = [prv] if rl is None else list(rl)
+    if _relays(topo, cores, nxt, cores[(j + 2) % N]) is not None and topo.may_write(nxt, d):
+        fs = [nxt] + fs
+    cut = [128 * i // len(fs) // 16 * 16 for i in range(len(fs))] + [128]
+    return [(f, cut[i], cut[i + 1]) for i, f in enumerate(fs)]
+
+
 def rank_program(g, core, T, topo):
     cores = list(T.cores)
     sem = T.sem
+    ve = g.vector
 
     def put(dst, out_ap, in_ap, rsem, lsem):
         rid, pid, _se = topo.addr(dst)
@@ -64,6 +78,26 @@ def rank_program(g, core, T, topo):
     def plane(buf, h):
         return buf[:, HW * h:HW * h + HW]
 
+    def feed_s3():
+        ve.memset(T.o_sb[:], 1.0).then_inc(sem.e1, 1)
+        ve.memset(T.e_sb[:], 0.0).then_inc(sem.e1, 1)
+        g.wait_ge(sem.e1, 2)
+        g.affine_select(T.o_sb[:], T.o_sb[:], [[-1, 128]], AluOpType.is_equal, 0.0, 0, 1).then_inc(sem.e2, 1)
+        ve.wait_ge(sem.e1, 2)
+        ve.wait_ge(sem.e2, 1)
+        ve.tensor_copy(T.e_sb[:, 3:515:4], T.o_sb[:]).then_inc(sem.e3, 1)
+        ve.wait_ge(sem.e3, 1)
+        ve.quantize_mx(T.qs[:, 384:512], T.pS[:, 384:512], T.e_sb[:, 0:512]).then_inc(sem.qS3, 1)
+        g.wait_ge(sem.qS3, 1)
+        left = 0
+        for j in range(N):
+            for f, c0, c1 in _feeders(topo, cores, j):
+                if f == core:
+                    left += put(cores[j], T.qsi[:, c0:c1].bitcast(dt.uint8), T.qs[:, 384 + c0:384 + c1].bitcast(dt.uint8),
+                                sem.sS, sem.sSl)
+                    left += put(cores[j], T.psi[:, c0:c1], T.pS[:, 384 + c0:384 + c1], sem.sS, sem.sSl)
+        return left
+
     rank = T.rank_of(core)
     if rank is None:
         for i in range(N):
@@ -71,6 +105,7 @@ def rank_program(g, core, T, topo):
             rl = _relays(topo, cores, s, d)
             if rl is None or core not in rl:
                 continue
+            s_left = feed_s3()
             got = _engines(topo.mask(s, core))
             left = 0
             for k in (1, 2, 3):
@@ -82,9 +117,10 @@ def rank_program(g, core, T, topo):
                         v = plane(T["pi%d" % (k + 1)], h)
                     left += put(d, v, v, sem["in%d%d" % (k + 1, h)], sem.fwd)
             g.wait_ge(sem.fwd, left)
+            g.wait_ge(sem.sSl, s_left)
         return
 
-    te, ve, sc, sy = g.tensor, g.vector, g.scalar, g.sync
+    te, sc, sy = g.tensor, g.scalar, g.sync
     nxt, prv = cores[(rank + 1) % N], cores[(rank - 1) % N]
     out_rl = _relays(topo, cores, core, nxt)
     in_rl = _relays(topo, cores, prv, core)
@@ -97,15 +133,16 @@ def rank_program(g, core, T, topo):
     else:
         tgt = out_rl
     sent_tot = 2 * (_engines(topo.mask(core, tgt[0])) + _engines(topo.mask(core, tgt[1])))
+    s3_in = sum(2 * _engines(topo.mask(f, core)) for f, _c0, _c1 in _feeders(topo, cores, rank))
     chain = [None] + [(rank - k) % N for k in (1, 2, 3, 4)]
 
     def load_b(k, lo, hi, s):
         c0 = 1024 * chain[k]
         sy.dma_start(T.b_sb[:, c0 + lo:c0 + hi], T.b[:, c0 + lo:c0 + hi]).then_inc(s, 16)
 
-    sy.dma_start(T.a_sb[:, 0:1024], T.a[:, 0:1024]).then_inc(sem.la0, 16)
-    sc.dma_start(T.a_sb[:, 1024:2048], T.a[:, 1024:2048]).then_inc(sem.la1, 16)
     load_b(1, 0, 512, sem.lb10)
+    sc.dma_start(T.a_sb[:, 0:1024], T.a[:, 0:1024]).then_inc(sem.la0, 16)
+    sy.dma_start(T.a_sb[:, 1024:2048], T.a[:, 1024:2048]).then_inc(sem.la1, 16)
     load_b(1, 512, 1024, sem.lb11)
     load_b(2, 0, 1024, sem.lb2)
     sy.wait_ge(sem.sent1, sent_tot)
@@ -113,9 +150,7 @@ def rank_program(g, core, T, topo):
     sy.wait_ge(sem.sent2, sent_tot)
     load_b(4, 0, 1024, sem.lb4)
 
-    ve.memset(T.e_sb[:], 1.0).then_inc(sem.e1, 1)
-    g.wait_ge(sem.e1, 1)
-    g.affine_select(T.e_sb[:], T.e_sb[:], [[-1, 516]], AluOpType.is_equal, 0.0, 3, 4).then_inc(sem.e2, 1)
+    s_left = feed_s3()
 
     def quant_b(k, lo, hi, ls, qsem):
         w0 = NC * chain[k]
@@ -123,18 +158,22 @@ def rank_program(g, core, T, topo):
         ve.quantize_mx(T.qb[:, w0 + lo:w0 + hi], T.pb[:, w0 + lo:w0 + hi],
                        T.b_sb[:, 4 * (w0 + lo):4 * (w0 + hi)]).then_inc(qsem, 1)
 
-    for j, (ls, qsem) in enumerate(((sem.la0, sem.qa0), (sem.la1, sem.qa1))):
-        ve.wait_ge(ls, 16)
-        ve.quantize_mx(T.qa[:, 256 * j:256 * j + 256], T.pa[:, 256 * j:256 * j + 256],
-                       T.a_sb[:, 1024 * j:1024 * j + 1024]).then_inc(qsem, 1)
+    def quant_a(lo, hi, qsem):
+        ve.quantize_mx(T.qa[:, lo:hi], T.pa[:, lo:hi], T.a_sb[:, 4 * lo:4 * hi]).then_inc(qsem, 1)
+
     quant_b(1, 0, HW, sem.lb10, sem.qb10)
+    ve.wait_ge(sem.la0, 16)
+    quant_a(0, 256, sem.qa0)
+    ve.wait_ge(sem.la1, 16)
+    quant_a(256, 384, sem.qa2)
+    quant_a(384, 512, sem.qa3)
     quant_b(1, HW, NC, sem.lb11, sem.qb11)
 
     st = {"gi": 0}
     reader = [None, None]
     mbc = [0] * 8
 
-    def group(lq, lp, rq, rp, n, pre):
+    def group(lhs, rq, rp, n, pre):
         gi = st["gi"]
         st["gi"] += 1
         s = gi % 2
@@ -147,12 +186,15 @@ def rank_program(g, core, T, topo):
             bank = 4 * s + b
             mbc[bank] += 1
             o = T.ps[:, 512 * bank:512 * bank + n]
-            te.matmul_mx(o, lq[:, 128 * b:128 * b + 128], lp[:, 128 * b:128 * b + 128], rq, rp,
-                         True, True).then_inc(sem["mb%d" % bank], 1)
+            te.matmul_mx(o, lhs[b][0], lhs[b][1], rq, rp, True, True).then_inc(sem["mb%d" % bank], 1)
             outs.append((o, sem["mb%d" % bank], mbc[bank]))
         rg = sem["rg%d" % gi]
         reader[s] = (rg, 4)
         return outs, rg
+
+    lhs_a = [(T.qa[:, 128 * b:128 * b + 128], T.pa[:, 128 * b:128 * b + 128]) for b in range(4)]
+    lhs_s = [(T.qs[:, 128 * b:128 * b + 128], T.pS[:, 128 * b:128 * b + 128]) for b in range(3)]
+    lhs_s.append((T.qsi[:, 0:128], T.psi[:, 0:128]))
 
     def send(k, h):
         g.wait_ge(sem["qt%d%d" % (k, h)], 1)
@@ -173,9 +215,9 @@ def rank_program(g, core, T, topo):
         pre = {0: [(sem["qb1%d" % h], 1)]}
         if h == 0:
             pre[0].append((sem.qa0, 1))
-            pre[2] = [(sem.qa1, 1)]
-        outs, rg = group(T.qa, T.pa, T.qb[:, w1 + HW * h:w1 + HW * h + HW], T.pb[:, w1 + HW * h:w1 + HW * h + HW],
-                         HW, pre)
+            pre[2] = [(sem.qa2, 1)]
+            pre[3] = [(sem.qa3, 1)]
+        outs, rg = group(lhs_a, T.qb[:, w1 + HW * h:w1 + HW * h + HW], T.pb[:, w1 + HW * h:w1 + HW * h + HW], HW, pre)
         for b, (o, ms, mc) in enumerate(outs):
             sc.wait_ge(ms, mc)
             sc.activation(T.t1[:, 512 * h + b:512 * h + 512:4], o, ActivationFunctionType.Relu,
@@ -184,15 +226,14 @@ def rank_program(g, core, T, topo):
     for h in (0, 1):
         quant_t(1, h, rgs[h])
 
-    ve.wait_ge(sem.e2, 1)
-    for b in range(4):
+    for b in range(3):
         ve.quantize_mx(T.qs[:, 128 * b:128 * b + 128], T.pS[:, 128 * b:128 * b + 128],
                        T.e_sb[:, 3 - b:3 - b + 512]).then_inc(sem.qS, 1)
 
     for k in (2, 3, 4):
         quant_b(k, 0, NC, sem["lb%d" % k], sem["qb%d" % k])
         wk = NC * chain[k]
-        outs, rgp = group(T.qa, T.pa, T.qb[:, wk:wk + NC], T.pb[:, wk:wk + NC], NC, {0: [(sem["qb%d" % k], 1)]})
+        outs, rgp = group(lhs_a, T.qb[:, wk:wk + NC], T.pb[:, wk:wk + NC], NC, {0: [(sem["qb%d" % k], 1)]})
         R = T["r%d" % k]
         for b, (o, ms, mc) in enumerate(outs):
             sc.wait_ge(ms, mc)
@@ -201,9 +242,9 @@ def rank_program(g, core, T, topo):
         for h in (0, 1):
             pre = {0: [(sem["in%d%d" % (k, h)], arrive)]}
             if k == 2 and h == 0:
-                pre[0].append((sem.qS, 4))
-            outs, rg = group(T.qs, T.pS, T["qi%d" % k][:, HW * h:HW * h + HW], T["pi%d" % k][:, HW * h:HW * h + HW],
-                             HW, pre)
+                pre[0].append((sem.qS, 3))
+                pre[3] = [(sem.sS, s3_in)]
+            outs, rg = group(lhs_s, T["qi%d" % k][:, HW * h:HW * h + HW], T["pi%d" % k][:, HW * h:HW * h + HW], HW, pre)
             if h == 0:
                 ve.wait_ge(rgp, 4)
             for b, (o, ms, mc) in enumerate(outs):
@@ -218,5 +259,6 @@ def rank_program(g, core, T, topo):
                     sem["st%d" % h], 16)
 
     g.wait_ge(sem.sent3, sent_tot)
+    g.wait_ge(sem.sSl, s_left)
     sy.wait_ge(sem.st0, 16)
     sy.wait_ge(sem.st1, 16)

from concourse.mybir import dt, AluOpType, ActivationFunctionType

N = 4
NC = 256
HW = 128
CSC = 0.023

SCRATCH = {
    "a_sb": ("sbuf", [128, 2048], "bfloat16"),
    "b_sb": ("sbuf", [128, 4096], "bfloat16"),
    "qa": ("sbuf", [128, 512], "float8_e4m3fn_x4"),
    "pa": ("sbuf", [128, 512], "uint8"),
    "qb": ("sbuf", [128, 1024], "float8_e4m3fn_x4"),
    "pb": ("sbuf", [128, 1024], "uint8"),
    "o_sb": ("sbuf", [128, 128], "bfloat16"),
    "e_sb": ("sbuf", [128, 516], "bfloat16"),
    "qs": ("sbuf", [128, 512], "float8_e4m3fn_x4"),
    "pS": ("sbuf", [128, 512], "uint8"),
    "qsi": ("sbuf", [128, 128], "float8_e4m3fn_x4"),
    "psi": ("sbuf", [128, 128], "uint8"),
    "y_sb": ("sbuf", [128, 1024], "float32"),
    "ps": ("psum", [128, 4096], "float32"),
}
for _k in (1, 2, 3):
    SCRATCH["t%d" % _k] = ("sbuf", [128, 1024], "bfloat16")
    SCRATCH["qt%d" % _k] = ("sbuf", [128, NC], "float8_e4m3fn_x4")
    SCRATCH["pt%d" % _k] = ("sbuf", [128, NC], "uint8")
    SCRATCH["r%d" % (_k + 1)] = ("sbuf", [128, 1024], "float32")
    SCRATCH["qi%d" % (_k + 1)] = ("sbuf", [128, NC], "float8_e4m3fn_x4")
    SCRATCH["pi%d" % (_k + 1)] = ("sbuf", [128, NC], "uint8")

SEMAPHORES = (["la0", "la1", "lb10", "lb11", "lb2", "lb3", "lb4", "e1", "e2", "e3", "qa0", "qa2", "qa3", "qb10", "qb11",
               "qb2", "qb3", "qb4", "qS", "qS3", "sS", "sSl", "st0", "st1", "sent1", "sent2", "sent3", "fwd"]
              + ["mb%d" % i for i in range(8)] + ["rg%d" % i for i in range(11)]
              + ["qt%d%d" % (k, h) for k in (1, 2, 3) for h in (0, 1)]
              + ["in%d%d" % (k, h) for k in (2, 3, 4) for h in (0, 1)]
              + ["rl%d%d" % (k, h) for k in (1, 2, 3) for h in (0, 1)])


def _engines(mask):
    return bin(mask).count("1")


def _relays(topo, cores, s, d):
    if topo.may_write(s, d):
        return None
    cand = [c for c in range(topo.CORES_PER_CHIP * topo.CHIPS)
            if topo.chip(c) == topo.chip(s) and c not in cores and topo.may_write(c, d)]
    cand.sort(key=lambda c: (topo.die(c) != topo.die(s), c))
    return cand[0], cand[1]


def _feeders(topo, cores, j):
    d, prv, nxt = cores[j], cores[(j - 1) % N], cores[(j + 1) % N]
    rl = _relays(topo, cores, prv, d)
    fs = [prv] if rl is None else list(rl)
    if _relays(topo, cores, nxt, cores[(j + 2) % N]) is not None and topo.may_write(nxt, d):
        fs = [nxt] + fs
    cut = [128 * i // len(fs) // 16 * 16 for i in range(len(fs))] + [128]
    return [(f, cut[i], cut[i + 1]) for i, f in enumerate(fs)]


def rank_program(g, core, T, topo):
    cores = list(T.cores)
    sem = T.sem
    ve = g.vector

    def put(dst, out_ap, in_ap, rsem, lsem):
        rid, pid, _se = topo.addr(dst)
        m = topo.mask(core, dst)
        g.remote_dma(out_ap=out_ap, in_ap=in_ap, remote_sem=rsem, local_sem=lsem, pid=pid, routing_id=rid,
                     dma_engine_mask=m)
        return _engines(m)

    def codes(buf, h):
        return buf[:, HW * h:HW * h + HW].bitcast(dt.uint8)

    def plane(buf, h):
        return buf[:, HW * h:HW * h + HW]

    def feed_s3():
        ve.memset(T.o_sb[:], 1.0).then_inc(sem.e1, 1)
        ve.memset(T.e_sb[:], 0.0).then_inc(sem.e1, 1)
        g.wait_ge(sem.e1, 2)
        g.affine_select(T.o_sb[:], T.o_sb[:], [[-1, 128]], AluOpType.is_equal, 0.0, 0, 1).then_inc(sem.e2, 1)
        ve.wait_ge(sem.e1, 2)
        ve.wait_ge(sem.e2, 1)
        ve.tensor_copy(T.e_sb[:, 3:515:4], T.o_sb[:]).then_inc(sem.e3, 1)
        ve.wait_ge(sem.e3, 1)
        ve.quantize_mx(T.qs[:, 384:512], T.pS[:, 384:512], T.e_sb[:, 0:512]).then_inc(sem.qS3, 1)
        g.wait_ge(sem.qS3, 1)
        left = 0
        for j in range(N):
            for f, c0, c1 in _feeders(topo, cores, j):
                if f == core:
                    left += put(cores[j], T.qsi[:, c0:c1].bitcast(dt.uint8), T.qs[:, 384 + c0:384 + c1].bitcast(dt.uint8),
                                sem.sS, sem.sSl)
                    left += put(cores[j], T.psi[:, c0:c1], T.pS[:, 384 + c0:384 + c1], sem.sS, sem.sSl)
        return left

    rank = T.rank_of(core)
    if rank is None:
        for i in range(N):
            s, d = cores[i], cores[(i + 1) % N]
            rl = _relays(topo, cores, s, d)
            if rl is None or core not in rl:
                continue
            s_left = feed_s3()
            got = _engines(topo.mask(s, core))
            left = 0
            for k in (1, 2, 3):
                for h in (0, 1):
                    g.wait_ge(sem["rl%d%d" % (k, h)], got)
                    if core == rl[0]:
                        v = codes(T["qi%d" % (k + 1)], h)
                    else:
                        v = plane(T["pi%d" % (k + 1)], h)
                    left += put(d, v, v, sem["in%d%d" % (k + 1, h)], sem.fwd)
            g.wait_ge(sem.fwd, left)
            g.wait_ge(sem.sSl, s_left)
        return

    te, sc, sy = g.tensor, g.scalar, g.sync
    nxt, prv = cores[(rank + 1) % N], cores[(rank - 1) % N]
    out_rl = _relays(topo, cores, core, nxt)
    in_rl = _relays(topo, cores, prv, core)
    if in_rl is None:
        arrive = 2 * _engines(topo.mask(prv, core))
    else:
        arrive = _engines(topo.mask(in_rl[0], core)) + _engines(topo.mask(in_rl[1], core))
    if out_rl is None:
        tgt = (nxt, nxt)
    else:
        tgt = out_rl
    sent_tot = 2 * (_engines(topo.mask(core, tgt[0])) + _engines(topo.mask(core, tgt[1])))
    s3_in = sum(2 * _engines(topo.mask(f, core)) for f, _c0, _c1 in _feeders(topo, cores, rank))
    chain = [None] + [(rank - k) % N for k in (1, 2, 3, 4)]

    def load_b(k, lo, hi, s):
        c0 = 1024 * chain[k]
        sy.dma_start(T.b_sb[:, c0 + lo:c0 + hi], T.b[:, c0 + lo:c0 + hi]).then_inc(s, 16)

    load_b(1, 0, 512, sem.lb10)
    sc.dma_start(T.a_sb[:, 0:1024], T.a[:, 0:1024]).then_inc(sem.la0, 16)
    sy.dma_start(T.a_sb[:, 1024:2048], T.a[:, 1024:2048]).then_inc(sem.la1, 16)
    load_b(1, 512, 1024, sem.lb11)
    load_b(2, 0, 1024, sem.lb2)
    sy.wait_ge(sem.sent1, sent_tot)
    load_b(3, 0, 1024, sem.lb3)
    sy.wait_ge(sem.sent2, sent_tot)
    load_b(4, 0, 1024, sem.lb4)

    s_left = feed_s3()

    def quant_b(k, lo, hi, ls, qsem):
        w0 = NC * chain[k]
        ve.wait_ge(ls, 16)
        ve.quantize_mx(T.qb[:, w0 + lo:w0 + hi], T.pb[:, w0 + lo:w0 + hi],
                       T.b_sb[:, 4 * (w0 + lo):4 * (w0 + hi)]).then_inc(qsem, 1)

    def quant_a(lo, hi, qsem):
        ve.quantize_mx(T.qa[:, lo:hi], T.pa[:, lo:hi], T.a_sb[:, 4 * lo:4 * hi]).then_inc(qsem, 1)

    quant_b(1, 0, HW, sem.lb10, sem.qb10)
    ve.wait_ge(sem.la0, 16)
    quant_a(0, 256, sem.qa0)
    ve.wait_ge(sem.la1, 16)
    quant_a(256, 384, sem.qa2)
    quant_a(384, 512, sem.qa3)
    quant_b(1, HW, NC, sem.lb11, sem.qb11)

    st = {"gi": 0}
    reader = [None, None]
    mbc = [0] * 8

    def group(lhs, rq, rp, n, pre):
        gi = st["gi"]
        st["gi"] += 1
        s = gi % 2
        if reader[s] is not None:
            te.wait_ge(reader[s][0], reader[s][1])
        outs = []
        for b in range(4):
            for w in pre.get(b, ()):
                te.wait_ge(w[0], w[1])
            bank = 4 * s + b
            mbc[bank] += 1
            o = T.ps[:, 512 * bank:512 * bank + n]
            te.matmul_mx(o, lhs[b][0], lhs[b][1], rq, rp, True, True).then_inc(sem["mb%d" % bank], 1)
            outs.append((o, sem["mb%d" % bank], mbc[bank]))
        rg = sem["rg%d" % gi]
        reader[s] = (rg, 4)
        return outs, rg

    lhs_a = [(T.qa[:, 128 * b:128 * b + 128], T.pa[:, 128 * b:128 * b + 128]) for b in range(4)]
    lhs_s = [(T.qs[:, 128 * b:128 * b + 128], T.pS[:, 128 * b:128 * b + 128]) for b in range(3)]
    lhs_s.append((T.qsi[:, 0:128], T.psi[:, 0:128]))

    def send(k, h):
        g.wait_ge(sem["qt%d%d" % (k, h)], 1)
        ls = sem["sent%d" % k]
        rs = sem["in%d%d" % (k + 1, h)] if out_rl is None else sem["rl%d%d" % (k, h)]
        put(tgt[0], codes(T["qi%d" % (k + 1)], h), codes(T["qt%d" % k], h), rs, ls)
        put(tgt[1], plane(T["pi%d" % (k + 1)], h), plane(T["pt%d" % k], h), rs, ls)

    def quant_t(k, h, rg):
        ve.wait_ge(rg, 4)
        ve.quantize_mx(T["qt%d" % k][:, HW * h:HW * h + HW], T["pt%d" % k][:, HW * h:HW * h + HW],
                       T["t%d" % k][:, 512 * h:512 * h + 512]).then_inc(sem["qt%d%d" % (k, h)], 1)
        send(k, h)

    w1 = NC * chain[1]
    rgs = []
    for h in (0, 1):
        pre = {0: [(sem["qb1%d" % h], 1)]}
        if h == 0:
            pre[0].append((sem.qa0, 1))
            pre[2] = [(sem.qa2, 1)]
            pre[3] = [(sem.qa3, 1)]
        outs, rg = group(lhs_a, T.qb[:, w1 + HW * h:w1 + HW * h + HW], T.pb[:, w1 + HW * h:w1 + HW * h + HW], HW, pre)
        for b, (o, ms, mc) in enumerate(outs):
            sc.wait_ge(ms, mc)
            sc.activation(T.t1[:, 512 * h + b:512 * h + 512:4], o, ActivationFunctionType.Relu,
                          scale=CSC).then_inc(rg, 1)
        rgs.append(rg)
    for h in (0, 1):
        quant_t(1, h, rgs[h])

    for b in range(3):
        ve.quantize_mx(T.qs[:, 128 * b:128 * b + 128], T.pS[:, 128 * b:128 * b + 128],
                       T.e_sb[:, 3 - b:3 - b + 512]).then_inc(sem.qS, 1)

    for k in (2, 3, 4):
        quant_b(k, 0, NC, sem["lb%d" % k], sem["qb%d" % k])
        wk = NC * chain[k]
        outs, rgp = group(lhs_a, T.qb[:, wk:wk + NC], T.pb[:, wk:wk + NC], NC, {0: [(sem["qb%d" % k], 1)]})
        R = T["r%d" % k]
        for b, (o, ms, mc) in enumerate(outs):
            sc.wait_ge(ms, mc)
            sc.activation(R[:, NC * b:NC * b + NC], o, ActivationFunctionType.Relu, scale=CSC).then_inc(rgp, 1)
        dst = T.y_sb if k == 4 else T["t%d" % k]
        for h in (0, 1):
            pre = {0: [(sem["in%d%d" % (k, h)], arrive)]}
            if k == 2 and h == 0:
                pre[0].append((sem.qS, 3))
                pre[3] = [(sem.sS, s3_in)]
            outs, rg = group(lhs_s, T["qi%d" % k][:, HW * h:HW * h + HW], T["pi%d" % k][:, HW * h:HW * h + HW], HW, pre)
            if h == 0:
                ve.wait_ge(rgp, 4)
            for b, (o, ms, mc) in enumerate(outs):
                ve.wait_ge(ms, mc)
                ve.tensor_tensor(dst[:, 512 * h + b:512 * h + 512:4], R[:, NC * b + HW * h:NC * b + HW * h + HW], o,
                                 AluOpType.add).then_inc(rg, 1)
            if k < 4:
                quant_t(k, h, rg)
            else:
                sy.wait_ge(rg, 4)
                sy.dma_start(T.y[:, 512 * h:512 * h + 512], T.y_sb[:, 512 * h:512 * h + 512]).then_inc(
                    sem["st%d" % h], 16)

    g.wait_ge(sem.sent3, sent_tot)
    g.wait_ge(sem.sSl, s_left)
    sy.wait_ge(sem.st0, 16)
    sy.wait_ge(sem.st1, 16)
